import numpy as np
import ml_dtypes


def mxq(x, axis, fmt="e4m3"):
    dtype, down = {"e4m3": (ml_dtypes.float8_e4m3fn, 7), "e5m2": (ml_dtypes.float8_e5m2, 14)}[fmt]
    v = np.moveaxis(np.asarray(x, np.float32).astype(ml_dtypes.bfloat16).astype(np.float64), axis, -1)
    blocks = v.reshape(v.shape[:-1] + (-1, 32))
    amax = np.abs(blocks).max(-1, keepdims=True)
    byte = np.maximum(np.where(amax > 0, np.frexp(amax)[1] - 1 + 127, 0) - down, 1)
    scale = np.exp2(byte - 127.0)
    codes = (blocks / scale).astype(np.float32).astype(dtype).astype(np.float64)
    return np.moveaxis((codes * scale).reshape(v.shape), -1, axis)


WIDE = False


def mx_kscale(k):
    if not WIDE:
        return np.ones(k)
    levels = np.array([10, -10, 5, -5, 0])
    if k % 512:
        return np.exp2(np.random.permutation(np.resize(levels, k // 32))).repeat(32)
    a = np.empty((k // 512, 16))
    for p in range(k // 512):
        a[p, :8] = np.random.permutation(np.resize(levels, 8))
        for g in range(8):
            far = levels[np.abs(levels - a[p, g]) >= 10]
            a[p, g + 8] = far[np.random.randint(len(far))]
    return np.exp2(a.ravel()).repeat(32)


def f64(x):
    return np.asarray(x).astype(np.float64)


def striped(idx):
    return np.tile(np.asarray(idx).reshape(-1, 16).T, (8, 1)).astype(np.uint16)


def unstriped(offs):
    return offs[:16].T.reshape(-1).astype(np.int64)


E2M1 = np.array([0.0, 0.5, 1.0, 1.5, 2.0, 3.0, 4.0, 6.0, -0.0, -0.5, -1.0, -1.5, -2.0, -3.0, -4.0, -6.0])


def pack_weight(w, fmt):
    k, n = w.shape
    w = f64(np.asarray(w, np.float32).astype(ml_dtypes.bfloat16)).reshape(k // 32, 32, n)
    amax = np.abs(w).max(1)
    if fmt == "e4m3":
        byte = np.frexp(amax)[1] - 1 + 127 - 7
    else:
        mant, ex = np.frexp(amax / 6.0)
        byte = np.where(mant > 0.5, ex, ex - 1) + 127
    byte = np.clip(np.where(amax > 0, byte, 1), 1, 254)
    scaled = (w * np.exp2(127.0 - byte)[:, None, :]).reshape(k, n).astype(np.float32)
    by_word = np.ascontiguousarray(scaled.reshape(k // 512, 128, 4, n).transpose(0, 1, 3, 2))
    if fmt == "e4m3":
        words = by_word.astype(ml_dtypes.float8_e4m3fn).view(np.uint8)
    else:
        c = by_word.astype(ml_dtypes.float4_e2m1fn).view(np.uint8) & 0xF
        words = (c[..., 0::2] | (c[..., 1::2] << 4)).reshape(k // 512, 128, 2 * n)
    return np.ascontiguousarray(words), np.ascontiguousarray(byte.astype(np.uint8).reshape(k // 512, 16, n))


def unpack_weight(words, scales, fmt):
    g, _, n = scales.shape
    words = np.ascontiguousarray(words).reshape(g, 128, n, -1)
    if fmt == "e4m3":
        vals = words.view(ml_dtypes.float8_e4m3fn).astype(np.float64)
    else:
        nib = np.empty((g, 128, n, 4), np.uint8)
        nib[..., 0::2] = words & 0xF
        nib[..., 1::2] = words >> 4
        vals = E2M1[nib]
    vals = vals * np.repeat(np.exp2(scales.astype(np.float64) - 127.0), 8, axis=1)[..., None]
    return vals.transpose(0, 1, 3, 2).reshape(g * 512, n)


K, S, T, N, L = 1024, 512, 512, 512, 512


def setup_inputs():
    n = np.random.standard_normal
    idx = np.random.randint(0, S, T)
    idx2 = np.random.randint(0, S, T)
    fk = mx_kscale(K)
    fl = mx_kscale(L)
    xbp = pack_weight(n((K, S)) / fk[:, None], "e4m3")
    xtp = pack_weight(n((L, T)) / fl[:, None], "e2m1")
    wtp = pack_weight(n((L, N)) * 1 / np.sqrt(L) * fl[:, None], "e4m3")
    return {
        "xb_words": xbp[0],
        "xb_scales": xbp[1],
        "wa": (n((K, N)) * 1 / np.sqrt(K) * fk[:, None]).astype(np.float32),
        "ga": (np.random.uniform(0.4, 1.0, (1, T))).astype(np.float32),
        "gb": (np.random.uniform(0.1, 0.6, (1, T))).astype(np.float32),
        "xt_words": xtp[0],
        "xt_scales": xtp[1],
        "wt_words": wtp[0],
        "wt_scales": wtp[1],
        "offs": striped(idx),
        "offs2": striped(idx2),
    }


def reference(xb_words, xb_scales, wa, ga, gb, xt_words, xt_scales, wt_words, wt_scales, offs, offs2):
    idx = unstriped(offs)
    idx2 = unstriped(offs2)
    xbu = unpack_weight(xb_words, xb_scales, "e4m3")
    xtu = unpack_weight(xt_words, xt_scales, "e2m1")
    wtu = unpack_weight(wt_words, wt_scales, "e4m3")
    waq = mxq(f64(wa), 0, "e4m3")
    z = waq.T @ xbu
    q = wtu.T @ xtu
    y = f64(ga) * z[:, idx] + f64(gb) * z[:, idx2] + q
    return y

@@ -1,0 +1,196 @@
+from contextlib import ExitStack
+
+import concourse.mybir as mybir
+from concourse.masks import make_identity
+
+K, S, T, N, L = 1024, 512, 512, 512, 512
+FLOPS = 2 * K * N * S + 2 * L * N * T
+
+F32 = mybir.dt.float32
+BF16 = mybir.dt.bfloat16
+I32 = mybir.dt.int32
+U32 = mybir.dt.uint32
+U16 = mybir.dt.uint16
+U8 = mybir.dt.uint8
+FP8X4 = mybir.dt.float8_e4m3fn_x4
+FP4X4 = mybir.dt.float4_e2m1fn_x4
+MULT = mybir.AluOpType.mult
+ADD = mybir.AluOpType.add
+
+P = 128
+PACK = 4
+PASSES = K // (P * PACK)
+BLOCKS = N // P
+SPARE = 16
+PE_BLOCKS = 3
+
+
+def tile_moe_buffer_read_twice_kernel(tc, xb_words, xb_scales, wa, ga, gb, xt_words, xt_scales, wt_words, wt_scales, offs, offs2, out):
+    nc = tc.nc
+    with ExitStack() as ctx:
+        keep = ctx.enter_context(tc.tile_pool(name="keep", bufs=1))
+        psum = ctx.enter_context(tc.psum_pool(name="psum", bufs=1))
+
+        def load_scales(plane, scales):
+            rows = scales.rearrange("z (q r) c -> r q z c", r=4)
+            for r in range(4):
+                nc.sync.dma_start(out=plane[r:P:32, :, :].bitcast(I32), in_=rows[r].bitcast(I32))
+
+        xb_plane = keep.tile([P, PASSES, S], U8, align_bytes=64)
+        xt_plane = keep.tile([P, 1, T], U8, align_bytes=64)
+        wt_plane = keep.tile([P, 1, N], U8, align_bytes=64)
+        nc.vector.memset(xb_plane[:].bitcast(I32), 0)
+        nc.vector.memset(xt_plane[:].bitcast(I32), 0)
+        nc.vector.memset(wt_plane[:].bitcast(I32), 0)
+
+        gate_cols = []
+        for name, gate in (("ga", ga), ("gb", gb)):
+            cols = keep.tile([P, PACK], F32, name=f"{name}_cols")
+            nc.sync.dma_start(out=cols[:], in_=gate.rearrange("o (p c) -> (o p) c", c=PACK))
+            gate_cols.append(cols)
+        ident = keep.tile([P, P], F32)
+        make_identity(nc, ident[:])
+        z = [keep.tile([P, S + SPARE], F32, name=f"z{j}") for j in range(BLOCKS)]
+        for j in range(BLOCKS):
+            nc.vector.memset(z[j][:, S:], 0.0)
+
+        wa_rows = wa.rearrange("(a p r) n -> a p r n", a=PASSES, r=PACK)
+        raw = {}
+
+        def load_wa(j0, j1):
+            for a in range(PASSES):
+                tile = keep.tile([P, PACK, (j1 - j0) * P], F32, name=f"wa_raw{j0}_{a}")
+                nc.sync.dma_start(out=tile[:], in_=wa_rows[a][:, :, j0 * P : j1 * P])
+                for j in range(j0, j1):
+                    raw[j, a] = tile[:, :, (j - j0) * P : (j - j0 + 1) * P]
+
+        load_wa(0, 2)
+        load_scales(xb_plane, xb_scales)
+        xb = []
+        for a in range(PASSES):
+            words = keep.tile([P, S], U32, name=f"xb{a}", align_bytes=64)
+            nc.sync.dma_start(out=words[:].bitcast(I32), in_=xb_words[a].rearrange("p s r -> p (s r)").bitcast(I32))
+            xb.append(words)
+        list_a = keep.tile([P, T // 16], U16)
+        nc.sync.dma_start(list_a[:], offs)
+        list_b = keep.tile([P, T // 16], U16)
+        nc.sync.dma_start(list_b[:], offs2)
+        load_wa(2, 3)
+        load_wa(3, 4)
+        xt = keep.tile([P, 2 * T], U8, align_bytes=64)
+        nc.sync.dma_start(out=xt[:].bitcast(I32), in_=xt_words[0].bitcast(I32))
+        wt = keep.tile([P, N], U32, align_bytes=64)
+        nc.sync.dma_start(out=wt[:].bitcast(I32), in_=wt_words[0].rearrange("p n r -> p (n r)").bitcast(I32))
+        load_scales(xt_plane, xt_scales)
+        load_scales(wt_plane, wt_scales)
+
+        grouped, codes, planes = {}, {}, {}
+
+        def cast(j, a, copy):
+            tile = keep.tile([P, P, PACK], BF16, name=f"wa_bf{j}_{a}", tag=f"wa_bf{j}_{a}", align_bytes=64)
+            copy(out=tile[:].rearrange("p (c i) r -> p c r i", i=4), in_=raw[j, a].rearrange("p r (c i) -> p c r i", i=4))
+            grouped[j, a] = tile
+
+        def quantize(j, a):
+            codes[j, a] = keep.tile([P, P], U32, name=f"wa_codes{j}_{a}", align_bytes=64)
+            planes[j, a] = keep.tile([P, P], U8, name=f"wa_plane{j}_{a}", align_bytes=64)
+            nc.vector.quantize_mx(out=codes[j, a][:].bitcast(FP8X4), scales=planes[j, a][:], in_=grouped[j, a][:].rearrange("p n r -> p (n r)"))
+
+        def z_pass(j, a, dst, cols):
+            nc.tensor.matmul_mx(out=dst, lhsT=codes[j, a][:].bitcast(FP8X4), lhsT_scale=planes[j, a][:],
+                                rhs=xb[a][:, cols].bitcast(FP8X4), rhs_scale=xb_plane[:, a, cols],
+                                start=(a == 0), stop=(a == PASSES - 1))
+
+        def bank(b):
+            return psum.tile([P, 512], F32, name=f"bank{b}", tag=f"bank{b}")
+
+        gates = []
+
+        def spread_gate(g):
+            spread = bank(2 + g)
+            for c in range(PACK):
+                nc.tensor.transpose(spread[:, c * P : (c + 1) * P], gate_cols[g][:, c : c + 1].to_broadcast([P, P]), ident[:])
+            rows = keep.tile([P, T], F32, name=f"gate_rows{g}")
+            nc.scalar.copy(out=rows[:].rearrange("m (p c) -> m p c", c=PACK), in_=spread[:].rearrange("m (c p) -> m p c", c=PACK))
+            gates.append(rows)
+
+        for a in range(PASSES):
+            cast(0, a, nc.vector.tensor_copy)
+            cast(1, a, nc.scalar.copy)
+            spread_gate(a)
+        for j in range(2):
+            for a in range(PASSES):
+                quantize(j, a)
+        half = S // 2
+        lo, hi = bank(0), bank(1)
+        for a in range(PASSES):
+            for h, b in enumerate((lo, hi)):
+                z_pass(0, a, b[:, :half], slice(h * half, (h + 1) * half))
+        nc.scalar.copy(out=z[0][:, :half], in_=lo[:, :half])
+        nc.vector.tensor_copy(out=z[0][:, half:S], in_=hi[:, :half])
+
+        z_banks = {1: 4, 2: 0, 3: 1}
+        for j in range(1, BLOCKS):
+            if j > 1:
+                for a in range(PASSES):
+                    cast(j, a, nc.scalar.copy)
+                for a in range(PASSES):
+                    quantize(j, a)
+            b = bank(z_banks[j])
+            for a in range(PASSES):
+                z_pass(j, a, b[:], slice(0, S))
+            nc.scalar.copy(out=z[j][:, :S], in_=b[:])
+
+        q_banks = []
+        for j in range(BLOCKS):
+            b = bank(2 + j)
+            nc.tensor.matmul_mx(out=b[:], lhsT=wt[:, j * P : (j + 1) * P].bitcast(FP8X4), lhsT_scale=wt_plane[:, 0, j * P : (j + 1) * P],
+                                rhs=xt[:].bitcast(FP4X4), rhs_scale=xt_plane[:, 0, :], start=True, stop=True)
+            q_banks.append(b)
+
+        def turn(dst, srcs):
+            for i, src in enumerate(srcs):
+                for c in range(4):
+                    nc.tensor.matmul(dst[:, c * P : (c + 1) * P], src[:, c * P : (c + 1) * P], ident[:], is_transpose=True,
+                                     start=(i == 0 and c == 0), stop=(i == len(srcs) - 1 and c == 3))
+
+        held = {"first1": "wa_bf2_0", "second1": "wa_bf2_1", "first2": "wa_bf3_0", "second2": "wa_bf3_1"}
+
+        def picked(name):
+            return keep.tile([P, T], F32, name=name, tag=held.get(name, name), align_bytes=64)
+
+        q_sb = {}
+        for j in range(PE_BLOCKS):
+            q_sb[j] = keep.tile([P, T], F32, name=f"q_sb{j}")
+            nc.scalar.copy(out=q_sb[j][:], in_=q_banks[j][:])
+
+        def finish(j):
+            first = picked(f"first{j}")
+            second = picked(f"second{j}")
+            result = keep.tile([P, T], F32, name=f"result{j}")
+            nc.vector.tensor_tensor(first[:], z[j][:].indirect(list_a[:]), gates[0][:], MULT)
+            if j < PE_BLOCKS:
+                nc.vector.tensor_tensor(second[:], z[j][:].indirect(list_b[:]), gates[1][:], MULT)
+                turned = bank(6)
+                turn(turned, [q_sb[j], first, second])
+                turned_sb = keep.tile([P, T], F32, name=f"turned_sb{j}")
+                nc.scalar.copy(out=turned_sb[:], in_=turned[:])
+                back = bank((7, 2, 7)[j])
+                turn(back, [turned_sb])
+                nc.scalar.copy(out=result[:], in_=back[:])
+                nc.sync.dma_start(out=out[j * P : (j + 1) * P, :], in_=result[:])
+            else:
+                partial = keep.tile([P, T], F32, name=f"partial{j}")
+                pieces = 2 if j == BLOCKS - 1 else 1
+                width = T // pieces
+                nc.vector.tensor_tensor(partial[:], first[:], q_banks[j][:], ADD)
+                for i in range(pieces):
+                    cols = slice(i * width, (i + 1) * width)
+                    nc.vector.tensor_tensor(second[:, cols], z[j][:].indirect(list_b[:, i * width // 16 : (i + 1) * width // 16]), gates[1][:, cols], MULT)
+                for i in range(pieces):
+                    cols = slice(i * width, (i + 1) * width)
+                    nc.vector.tensor_tensor(result[:, cols], partial[:, cols], second[:, cols], ADD)
+                    nc.sync.dma_start(out=out[j * P : (j + 1) * P, cols], in_=result[:, cols])
+
+        for j in range(BLOCKS):
+            finish(j)

@@ -39,15 +39,18 @@ def tile_moe_buffer_read_twice_kernel(tc, xb_words, xb_scales, wa, ga, gb, xt_wo
         xb_plane = keep.tile([P, PASSES, S], U8, align_bytes=64)
         xt_plane = keep.tile([P, 1, T], U8, align_bytes=64)
         wt_plane = keep.tile([P, 1, N], U8, align_bytes=64)
-        nc.vector.memset(xb_plane[:].bitcast(I32), 0)
+        nc.gpsimd.memset(xb_plane[:].bitcast(I32), 0)
         nc.vector.memset(xt_plane[:].bitcast(I32), 0)
         nc.vector.memset(wt_plane[:].bitcast(I32), 0)
 
         gate_cols = []
-        for name, gate in (("ga", ga), ("gb", gb)):
-            cols = keep.tile([P, PACK], F32, name=f"{name}_cols")
+
+        def load_gate(name, gate):
+            cols = keep.tile([P, PACK], F32, name=f"{name}_cols", tag=("wa_bf1_0", "wa_bf2_0")[len(gate_cols)], align_bytes=64)
             nc.sync.dma_start(out=cols[:], in_=gate.rearrange("o (p c) -> (o p) c", c=PACK))
             gate_cols.append(cols)
+
+        load_gate("ga", ga)
         ident = keep.tile([P, P], F32)
         make_identity(nc, ident[:])
         z = [keep.tile([P, S + SPARE], F32, name=f"z{j}") for j in range(BLOCKS)]
@@ -73,6 +76,7 @@ def tile_moe_buffer_read_twice_kernel(tc, xb_words, xb_scales, wa, ga, gb, xt_wo
             xb.append(words)
         list_a = keep.tile([P, T // 16], U16)
         nc.sync.dma_start(list_a[:], offs)
+        load_gate("gb", gb)
         list_b = keep.tile([P, T // 16], U16)
         nc.sync.dma_start(list_b[:], offs2)
         load_wa(2, 3)
@@ -104,93 +108,87 @@ def tile_moe_buffer_read_twice_kernel(tc, xb_words, xb_scales, wa, ga, gb, xt_wo
         def bank(b):
             return psum.tile([P, 512], F32, name=f"bank{b}", tag=f"bank{b}")
 
+        def pair():
+            return psum.tile([P, 2, 512], F32, name="pair", tag="pair")
+
         gates = []
 
         def spread_gate(g):
-            spread = bank(2 + g)
+            spread = pair()[:, 0, :]
             for c in range(PACK):
                 nc.tensor.transpose(spread[:, c * P : (c + 1) * P], gate_cols[g][:, c : c + 1].to_broadcast([P, P]), ident[:])
             rows = keep.tile([P, T], F32, name=f"gate_rows{g}")
-            nc.scalar.copy(out=rows[:].rearrange("m (p c) -> m p c", c=PACK), in_=spread[:].rearrange("m (c p) -> m p c", c=PACK))
+            nc.scalar.copy(out=rows[:].rearrange("m (p c) -> m p c", c=PACK), in_=spread.rearrange("m (c p) -> m p c", c=PACK))
             gates.append(rows)
 
+        spread_gate(0)
         for a in range(PASSES):
             cast(0, a, nc.vector.tensor_copy)
             cast(1, a, nc.scalar.copy)
-            spread_gate(a)
         for j in range(2):
             for a in range(PASSES):
                 quantize(j, a)
         half = S // 2
-        lo, hi = bank(0), bank(1)
+        halves = pair()
         for a in range(PASSES):
-            for h, b in enumerate((lo, hi)):
-                z_pass(0, a, b[:, :half], slice(h * half, (h + 1) * half))
-        nc.scalar.copy(out=z[0][:, :half], in_=lo[:, :half])
-        nc.vector.tensor_copy(out=z[0][:, half:S], in_=hi[:, :half])
+            for h in range(2):
+                z_pass(0, a, halves[:, h, :half], slice(h * half, (h + 1) * half))
+        nc.scalar.copy(out=z[0][:, :half], in_=halves[:, 0, :half])
+        nc.vector.tensor_copy(out=z[0][:, half:S], in_=halves[:, 1, :half])
 
-        z_banks = {1: 4, 2: 0, 3: 1}
         for j in range(1, BLOCKS):
             if j > 1:
                 for a in range(PASSES):
                     cast(j, a, nc.scalar.copy)
                 for a in range(PASSES):
                     quantize(j, a)
-            b = bank(z_banks[j])
+            b = bank(2)[:] if j == 1 else pair()[:, 0, :]
             for a in range(PASSES):
-                z_pass(j, a, b[:], slice(0, S))
-            nc.scalar.copy(out=z[j][:, :S], in_=b[:])
+                z_pass(j, a, b, slice(0, S))
+            nc.scalar.copy(out=z[j][:, :S], in_=b)
+            if j == 1:
+                spread_gate(1)
 
-        q_banks = []
+        q = []
         for j in range(BLOCKS):
-            b = bank(2 + j)
-            nc.tensor.matmul_mx(out=b[:], lhsT=wt[:, j * P : (j + 1) * P].bitcast(FP8X4), lhsT_scale=wt_plane[:, 0, j * P : (j + 1) * P],
+            b = bank(3 + j)[:]
+            nc.tensor.matmul_mx(out=b, lhsT=wt[:, j * P : (j + 1) * P].bitcast(FP8X4), lhsT_scale=wt_plane[:, 0, j * P : (j + 1) * P],
                                 rhs=xt[:].bitcast(FP4X4), rhs_scale=xt_plane[:, 0, :], start=True, stop=True)
-            q_banks.append(b)
+            q.append(b)
 
-        def turn(dst, srcs):
-            for i, src in enumerate(srcs):
-                for c in range(4):
-                    nc.tensor.matmul(dst[:, c * P : (c + 1) * P], src[:, c * P : (c + 1) * P], ident[:], is_transpose=True,
-                                     start=(i == 0 and c == 0), stop=(i == len(srcs) - 1 and c == 3))
+        held = {(0, 1): "wa_bf2_0", (1, 1): "wa_bf2_1", (2, 0): "wa_bf3_1", (3, 0): "both1", (3, 1): "both2"}
+        picked, both = {}, {}
 
-        held = {"first1": "wa_bf2_0", "second1": "wa_bf2_1", "first2": "wa_bf3_0", "second2": "wa_bf3_1"}
+        def pick(j, g):
+            name = f"picked{j}_{g}"
+            picked[j, g] = keep.tile([P, T], F32, name=name, tag=held.get((j, g), name), align_bytes=64)
+            nc.vector.tensor_tensor(picked[j, g][:], z[j][:].indirect((list_a, list_b)[g][:]), gates[g][:], MULT)
 
-        def picked(name):
-            return keep.tile([P, T], F32, name=name, tag=held.get(name, name), align_bytes=64)
+        def join(j):
+            both[j] = keep.tile([P, T], F32, name=f"both{j}", tag=f"both{j}", align_bytes=64)
+            nc.vector.tensor_tensor(both[j][:], picked[j, 0][:], picked[j, 1][:], ADD)
 
-        q_sb = {}
-        for j in range(PE_BLOCKS):
-            q_sb[j] = keep.tile([P, T], F32, name=f"q_sb{j}")
-            nc.scalar.copy(out=q_sb[j][:], in_=q_banks[j][:])
-
-        def finish(j):
-            first = picked(f"first{j}")
-            second = picked(f"second{j}")
+        def finish(j, first, second, pieces):
             result = keep.tile([P, T], F32, name=f"result{j}")
-            nc.vector.tensor_tensor(first[:], z[j][:].indirect(list_a[:]), gates[0][:], MULT)
-            if j < PE_BLOCKS:
-                nc.vector.tensor_tensor(second[:], z[j][:].indirect(list_b[:]), gates[1][:], MULT)
-                turned = bank(6)
-                turn(turned, [q_sb[j], first, second])
-                turned_sb = keep.tile([P, T], F32, name=f"turned_sb{j}")
-                nc.scalar.copy(out=turned_sb[:], in_=turned[:])
-                back = bank((7, 2, 7)[j])
-                turn(back, [turned_sb])
-                nc.scalar.copy(out=result[:], in_=back[:])
-                nc.sync.dma_start(out=out[j * P : (j + 1) * P, :], in_=result[:])
-            else:
-                partial = keep.tile([P, T], F32, name=f"partial{j}")
-                pieces = 2 if j == BLOCKS - 1 else 1
-                width = T // pieces
-                nc.vector.tensor_tensor(partial[:], first[:], q_banks[j][:], ADD)
-                for i in range(pieces):
-                    cols = slice(i * width, (i + 1) * width)
-                    nc.vector.tensor_tensor(second[:, cols], z[j][:].indirect(list_b[:, i * width // 16 : (i + 1) * width // 16]), gates[1][:, cols], MULT)
-                for i in range(pieces):
-                    cols = slice(i * width, (i + 1) * width)
-                    nc.vector.tensor_tensor(result[:, cols], partial[:, cols], second[:, cols], ADD)
-                    nc.sync.dma_start(out=out[j * P : (j + 1) * P, cols], in_=result[:, cols])
+            for i in range(pieces):
+                cols = slice(i * T // pieces, (i + 1) * T // pieces)
+                nc.vector.tensor_tensor(result[:, cols], first[:, cols], second[:, cols], ADD)
+                nc.sync.dma_start(out=out[j * P : (j + 1) * P, cols], in_=result[:, cols])
 
-        for j in range(BLOCKS):
-            finish(j)
+        pick(0, 0)
+        pick(1, 0)
+        pick(0, 1)
+        pick(1, 1)
+        join(0)
+        join(1)
+        pick(2, 0)
+        pick(2, 1)
+        finish(0, q[0], both[0][:], 1)
+        join(2)
+        finish(1, q[1], both[1][:], 1)
+        pick(3, 0)
+        finish(2, q[2], both[2][:], 1)
+        partial = keep.tile([P, T], F32)
+        nc.vector.tensor_tensor(partial[:], q[3], picked[3, 0][:], ADD)
+        pick(3, 1)
+        finish(3, partial[:], picked[3, 1][:], 2)

from contextlib import ExitStack

import concourse.mybir as mybir
from concourse.masks import make_identity

K, S, T, N, L = 1024, 512, 512, 512, 512
FLOPS = 2 * K * N * S + 2 * L * N * T

F32 = mybir.dt.float32
BF16 = mybir.dt.bfloat16
I32 = mybir.dt.int32
U32 = mybir.dt.uint32
U16 = mybir.dt.uint16
U8 = mybir.dt.uint8
FP8X4 = mybir.dt.float8_e4m3fn_x4
FP4X4 = mybir.dt.float4_e2m1fn_x4
MULT = mybir.AluOpType.mult
ADD = mybir.AluOpType.add

P = 128
PACK = 4
PASSES = K // (P * PACK)
BLOCKS = N // P
SPARE = 16
PE_BLOCKS = 3


def tile_moe_buffer_read_twice_kernel(tc, xb_words, xb_scales, wa, ga, gb, xt_words, xt_scales, wt_words, wt_scales, offs, offs2, out):
    nc = tc.nc
    with ExitStack() as ctx:
        keep = ctx.enter_context(tc.tile_pool(name="keep", bufs=1))
        psum = ctx.enter_context(tc.psum_pool(name="psum", bufs=1))

        def load_scales(plane, scales):
            rows = scales.rearrange("z (q r) c -> r q z c", r=4)
            for r in range(4):
                nc.sync.dma_start(out=plane[r:P:32, :, :].bitcast(I32), in_=rows[r].bitcast(I32))

        xb_plane = keep.tile([P, PASSES, S], U8, align_bytes=64)
        xt_plane = keep.tile([P, 1, T], U8, align_bytes=64)
        wt_plane = keep.tile([P, 1, N], U8, align_bytes=64)
        nc.gpsimd.memset(xb_plane[:].bitcast(I32), 0)
        nc.vector.memset(xt_plane[:].bitcast(I32), 0)
        nc.vector.memset(wt_plane[:].bitcast(I32), 0)

        gate_cols = []

        def load_gate(name, gate):
            cols = keep.tile([P, PACK], F32, name=f"{name}_cols", tag=("wa_bf1_0", "wa_bf2_0")[len(gate_cols)], align_bytes=64)
            nc.sync.dma_start(out=cols[:], in_=gate.rearrange("o (p c) -> (o p) c", c=PACK))
            gate_cols.append(cols)

        load_gate("ga", ga)
        ident = keep.tile([P, P], F32)
        make_identity(nc, ident[:])
        z = [keep.tile([P, S + SPARE], F32, name=f"z{j}") for j in range(BLOCKS)]
        for j in range(BLOCKS):
            nc.vector.memset(z[j][:, S:], 0.0)

        wa_rows = wa.rearrange("(a p r) n -> a p r n", a=PASSES, r=PACK)
        raw = {}

        def load_wa(j0, j1):
            for a in range(PASSES):
                tile = keep.tile([P, PACK, (j1 - j0) * P], F32, name=f"wa_raw{j0}_{a}")
                nc.sync.dma_start(out=tile[:], in_=wa_rows[a][:, :, j0 * P : j1 * P])
                for j in range(j0, j1):
                    raw[j, a] = tile[:, :, (j - j0) * P : (j - j0 + 1) * P]

        load_wa(0, 2)
        load_scales(xb_plane, xb_scales)
        xb = []
        for a in range(PASSES):
            words = keep.tile([P, S], U32, name=f"xb{a}", align_bytes=64)
            nc.sync.dma_start(out=words[:].bitcast(I32), in_=xb_words[a].rearrange("p s r -> p (s r)").bitcast(I32))
            xb.append(words)
        list_a = keep.tile([P, T // 16], U16)
        nc.sync.dma_start(list_a[:], offs)
        load_gate("gb", gb)
        list_b = keep.tile([P, T // 16], U16)
        nc.sync.dma_start(list_b[:], offs2)
        load_wa(2, 3)
        load_wa(3, 4)
        xt = keep.tile([P, 2 * T], U8, align_bytes=64)
        nc.sync.dma_start(out=xt[:].bitcast(I32), in_=xt_words[0].bitcast(I32))
        wt = keep.tile([P, N], U32, align_bytes=64)
        nc.sync.dma_start(out=wt[:].bitcast(I32), in_=wt_words[0].rearrange("p n r -> p (n r)").bitcast(I32))
        load_scales(xt_plane, xt_scales)
        load_scales(wt_plane, wt_scales)

        grouped, codes, planes = {}, {}, {}

        def cast(j, a, copy):
            tile = keep.tile([P, P, PACK], BF16, name=f"wa_bf{j}_{a}", tag=f"wa_bf{j}_{a}", align_bytes=64)
            copy(out=tile[:].rearrange("p (c i) r -> p c r i", i=4), in_=raw[j, a].rearrange("p r (c i) -> p c r i", i=4))
            grouped[j, a] = tile

        def quantize(j, a):
            codes[j, a] = keep.tile([P, P], U32, name=f"wa_codes{j}_{a}", align_bytes=64)
            planes[j, a] = keep.tile([P, P], U8, name=f"wa_plane{j}_{a}", align_bytes=64)
            nc.vector.quantize_mx(out=codes[j, a][:].bitcast(FP8X4), scales=planes[j, a][:], in_=grouped[j, a][:].rearrange("p n r -> p (n r)"))

        def z_pass(j, a, dst, cols):
            nc.tensor.matmul_mx(out=dst, lhsT=codes[j, a][:].bitcast(FP8X4), lhsT_scale=planes[j, a][:],
                                rhs=xb[a][:, cols].bitcast(FP8X4), rhs_scale=xb_plane[:, a, cols],
                                start=(a == 0), stop=(a == PASSES - 1))

        def bank(b):
            return psum.tile([P, 512], F32, name=f"bank{b}", tag=f"bank{b}")

        def pair():
            return psum.tile([P, 2, 512], F32, name="pair", tag="pair")

        gates = []

        def spread_gate(g):
            spread = pair()[:, 0, :]
            for c in range(PACK):
                nc.tensor.transpose(spread[:, c * P : (c + 1) * P], gate_cols[g][:, c : c + 1].to_broadcast([P, P]), ident[:])
            rows = keep.tile([P, T], F32, name=f"gate_rows{g}")
            nc.scalar.copy(out=rows[:].rearrange("m (p c) -> m p c", c=PACK), in_=spread.rearrange("m (c p) -> m p c", c=PACK))
            gates.append(rows)

        spread_gate(0)
        for a in range(PASSES):
            cast(0, a, nc.vector.tensor_copy)
            cast(1, a, nc.scalar.copy)
        for j in range(2):
            for a in range(PASSES):
                quantize(j, a)
        half = S // 2
        halves = pair()
        for a in range(PASSES):
            for h in range(2):
                z_pass(0, a, halves[:, h, :half], slice(h * half, (h + 1) * half))
        nc.scalar.copy(out=z[0][:, :half], in_=halves[:, 0, :half])
        nc.vector.tensor_copy(out=z[0][:, half:S], in_=halves[:, 1, :half])

        for j in range(1, BLOCKS):
            if j > 1:
                for a in range(PASSES):
                    cast(j, a, nc.scalar.copy)
                for a in range(PASSES):
                    quantize(j, a)
            b = bank(2)[:] if j == 1 else pair()[:, 0, :]
            for a in range(PASSES):
                z_pass(j, a, b, slice(0, S))
            nc.scalar.copy(out=z[j][:, :S], in_=b)
            if j == 1:
                spread_gate(1)

        q = []
        for j in range(BLOCKS):
            b = bank(3 + j)[:]
            nc.tensor.matmul_mx(out=b, lhsT=wt[:, j * P : (j + 1) * P].bitcast(FP8X4), lhsT_scale=wt_plane[:, 0, j * P : (j + 1) * P],
                                rhs=xt[:].bitcast(FP4X4), rhs_scale=xt_plane[:, 0, :], start=True, stop=True)
            q.append(b)

        held = {(0, 1): "wa_bf2_0", (1, 1): "wa_bf2_1", (2, 0): "wa_bf3_1", (3, 0): "both1", (3, 1): "both2"}
        picked, both = {}, {}

        def pick(j, g):
            name = f"picked{j}_{g}"
            picked[j, g] = keep.tile([P, T], F32, name=name, tag=held.get((j, g), name), align_bytes=64)
            nc.vector.tensor_tensor(picked[j, g][:], z[j][:].indirect((list_a, list_b)[g][:]), gates[g][:], MULT)

        def join(j):
            both[j] = keep.tile([P, T], F32, name=f"both{j}", tag=f"both{j}", align_bytes=64)
            nc.vector.tensor_tensor(both[j][:], picked[j, 0][:], picked[j, 1][:], ADD)

        def finish(j, first, second, pieces):
            result = keep.tile([P, T], F32, name=f"result{j}")
            for i in range(pieces):
                cols = slice(i * T // pieces, (i + 1) * T // pieces)
                nc.vector.tensor_tensor(result[:, cols], first[:, cols], second[:, cols], ADD)
                nc.sync.dma_start(out=out[j * P : (j + 1) * P, cols], in_=result[:, cols])

        pick(0, 0)
        pick(1, 0)
        pick(0, 1)
        pick(1, 1)
        join(0)
        join(1)
        pick(2, 0)
        pick(2, 1)
        finish(0, q[0], both[0][:], 1)
        join(2)
        finish(1, q[1], both[1][:], 1)
        pick(3, 0)
        finish(2, q[2], both[2][:], 1)
        partial = keep.tile([P, T], F32)
        nc.vector.tensor_tensor(partial[:], q[3], picked[3, 0][:], ADD)
        pick(3, 1)
        finish(3, partial[:], picked[3, 1][:], 2)
